import numpy as np
import ml_dtypes


def mxq(x, axis, fmt="e4m3"):
    dtype, down = {"e4m3": (ml_dtypes.float8_e4m3fn, 7), "e5m2": (ml_dtypes.float8_e5m2, 14)}[fmt]
    v = np.moveaxis(np.asarray(x, np.float32).astype(ml_dtypes.bfloat16).astype(np.float64), axis, -1)
    blocks = v.reshape(v.shape[:-1] + (-1, 32))
    amax = np.abs(blocks).max(-1, keepdims=True)
    byte = np.maximum(np.where(amax > 0, np.frexp(amax)[1] - 1 + 127, 0) - down, 1)
    scale = np.exp2(byte - 127.0)
    codes = (blocks / scale).astype(np.float32).astype(dtype).astype(np.float64)
    return np.moveaxis((codes * scale).reshape(v.shape), -1, axis)


WIDE = False


def mx_kscale(k):
    if not WIDE:
        return np.ones(k)
    levels = np.array([10, -10, 5, -5, 0])
    if k % 512:
        return np.exp2(np.random.permutation(np.resize(levels, k // 32))).repeat(32)
    a = np.empty((k // 512, 16))
    for p in range(k // 512):
        a[p, :8] = np.random.permutation(np.resize(levels, 8))
        for g in range(8):
            far = levels[np.abs(levels - a[p, g]) >= 10]
            a[p, g + 8] = far[np.random.randint(len(far))]
    return np.exp2(a.ravel()).repeat(32)


BF16 = ml_dtypes.bfloat16


def bf(x):
    return np.asarray(x, np.float32).astype(BF16)


def f64(x):
    return np.asarray(x).astype(np.float64)

def planes(Y):
    n, m = Y.shape
    b = f64(bf(Y)).reshape(n // 32, 32, m)
    amax = np.abs(b).max(1)
    byte = np.clip(np.where(amax > 0, np.frexp(amax)[1] - 1 + 127 - 7, 1), 1, 254)
    codes = (b * np.exp2(127.0 - byte)[:, None, :]).reshape(n, m).astype(np.float32).astype(ml_dtypes.float8_e4m3fn).view(np.uint8)
    words = codes.reshape(n // 512, 128, 4, m).transpose(0, 1, 3, 2)
    return np.ascontiguousarray(words), np.ascontiguousarray(byte.astype(np.uint8).reshape(n // 512, 16, m))


N, M, D = 1024, 1024, 1024


def sigmoid(a):
    return 1.0 / (1.0 + np.exp(-a))


def setup_inputs():
    s, t = mx_kscale(D), mx_kscale(M)
    return {"z": bf(np.random.standard_normal((N, D)) * s[None, :]),
            "y": bf(np.random.standard_normal((M, D))),
            "adj": bf(np.random.uniform(0.0, 1.0, (N, M))),
            "g": bf((1.0 + 0.1 * np.random.standard_normal(D)) / s),
            "bj": bf(0.5 * np.random.standard_normal(M)),
            "v": bf((1.0 + 0.1 * np.random.standard_normal(M)) * t),
            "r": bf((1.0 + 0.1 * np.random.standard_normal(M)) / t)}


def core(z, y, adj, g, bj, v, r):
    z, y, adj, g, bj, v, r = f64(z), f64(y), f64(adj), f64(g), f64(bj), f64(v), f64(r)
    d = z.shape[1]
    m = y.shape[0]
    yg = y * g[None, :]
    sc = mxq(z, 1, "e4m3") @ mxq(yg, 1, "e4m3").T
    pr = sigmoid(sc / np.sqrt(d) + bj[None, :])
    res = (pr - adj) * v[None, :]
    yr = y * r[:, None]
    return (mxq(res, 1, "e4m3") @ mxq(yr, 0, "e4m3")) / np.sqrt(m)


def reference(z, y, adj, g, bj, v, r):
    R_out = core(z, y, adj, g, bj, v, r)
    words, scales = planes(R_out.T)
    return R_out, words, scales

@@ -1,0 +1,287 @@
+from contextlib import ExitStack
+
+import concourse.mybir as mybir
+from concourse.masks import make_identity
+
+N, M, D = 1024, 1024, 1024
+FLOPS = 2 * N * M * D + 2 * N * M * D
+
+F32 = mybir.dt.float32
+BF16 = mybir.dt.bfloat16
+U32 = mybir.dt.uint32
+I32 = mybir.dt.int32
+U8 = mybir.dt.uint8
+FP8X4 = mybir.dt.float8_e4m3fn_x4
+ACT = mybir.ActivationFunctionType
+ALU = mybir.AluOpType
+
+P = 128
+CH = 256
+NCH = N // CH
+
+
+def tile_innerproductsigmoidresidualprojection_kernel(tc, z, y, adj, g, bj, v, r, out_0, out_1, out_2):
+    nc = tc.nc
+    with ExitStack() as ctx:
+        keep = ctx.enter_context(tc.tile_pool(name="keep", bufs=1))
+        work = ctx.enter_context(tc.tile_pool(name="work", bufs=2))
+        psum = ctx.enter_context(tc.psum_pool(name="psum", bufs=2))
+
+        y_raw = {}
+        z_raw = {}
+        a_raw = {}
+        for G in range(2):
+            for j in range(4):
+                y_raw[G, j] = keep.tile([P, D], BF16, name="y_raw_%d_%d" % (G, j), align_bytes=64)
+        for c in range(NCH):
+            z_raw[c] = keep.tile([P, 2, D], BF16, name="z_raw_%d" % c, align_bytes=64)
+            a_raw[c] = keep.tile([P, 2, M], BF16, name="a_raw_%d" % c, align_bytes=64)
+        vecs = {}
+        for name in ("r", "g", "bj", "v"):
+            vecs[name] = keep.tile([P, 2, 4], BF16, name="vec_" + name)
+        y_scaled = {}
+        yr_bf = {}
+        yr_codes = {}
+        yr_scales = {}
+        yg_bf = {}
+        yg_codes = {}
+        yg_scales = {}
+        for G in range(2):
+            y_scaled[G] = keep.tile([P, 4, D], BF16, name="y_scaled_%d" % G, align_bytes=64)
+            yr_bf[G] = keep.tile([P, D, 4], BF16, name="yr_bf_%d" % G, align_bytes=64)
+            yr_codes[G] = keep.tile([P, D], U32, name="yr_codes_%d" % G, align_bytes=64)
+            yr_scales[G] = keep.tile([P, D], U8, name="yr_scales_%d" % G, align_bytes=64)
+            yg_codes[G] = keep.tile([P, M], U32, name="yg_codes_%d" % G, align_bytes=64)
+            yg_scales[G] = keep.tile([P, M], U8, name="yg_scales_%d" % G, align_bytes=64)
+            for f in range(2):
+                yg_bf[G, f] = keep.tile([P, 512, 4], BF16, name="yg_bf_%d_%d" % (G, f), align_bytes=64)
+        out_scales = keep.tile([P, 2, N], U8, name="out_scales", align_bytes=64)
+        ident = keep.tile([P, P], F32, name="ident")
+        warm = keep.tile([P, 1], F32, name="warm")
+
+        def load_y(G):
+            src = y[512 * G : 512 * G + 512, :].rearrange("(p j) d -> p j d", j=4)
+            for j in range(4):
+                nc.sync.dma_start(out=y_raw[G, j][:], in_=src[:, j, :])
+
+        def load_rows(dst, src, c):
+            nc.sync.dma_start(out=dst[c][:], in_=src[CH * c : CH * c + CH, :].rearrange("(i p) k -> p i k", p=P))
+
+        t_y = {}
+        t_z = {}
+        t_a = {}
+        t_s = {}
+        t_o = {}
+        t_p = {}
+        z_bf = {}
+        z_codes = {}
+        z_scales = {}
+        pr = {}
+        dd = {}
+        res_bf = {}
+        res_codes = {}
+        res_scales = {}
+        of = {}
+        cast = {}
+        p_bf = {}
+        p_codes = {}
+
+        def Y(G, jp):
+            for f in range(2):
+                bank = psum.tile([P, 2, CH], F32, name="bank_tr", tag="tr")
+                t_y[G, jp, f] = bank
+                for k in range(2):
+                    words = y_raw[G, 2 * jp + k][:].bitcast(F32)
+                    for u in range(2):
+                        nc.tensor.transpose(bank[:, u, P * k : P * k + P], words[:, 256 * f + u : 256 * f + 256 : 2], ident[:])
+
+        def Ye(G, jp):
+            for f in range(2):
+                src = t_y[G, jp, f][:].rearrange("p u m -> p (u m)").bitcast(BF16).rearrange("p (u m e) -> p m u e", u=2, e=2)
+                dst = yg_bf[G, f][:, CH * jp : CH * jp + CH, :].rearrange("p m (u e) -> p m u e", u=2)
+                fac = vecs["g"][:, f, :].unsqueeze(1).to_broadcast([P, CH, 4]).rearrange("p m (u e) -> p m u e", u=2)
+                nc.vector.tensor_tensor(out=dst, in0=src, in1=fac, op=ALU.mult)
+
+        def Yq(G):
+            cols = slice(512 * G, 512 * G + 512)
+            for f in range(2):
+                nc.vector.quantize_mx(out=yg_codes[f][:, cols].bitcast(FP8X4), scales=yg_scales[f][:, cols], in_=yg_bf[G, f][:].rearrange("p m t -> p (m t)"))
+
+        def rows_to_banks(raw, store, c, tag):
+            for f in range(2):
+                bank = psum.tile([P, 2, CH], F32, name="bank_" + tag, tag=tag)
+                store[c, f] = bank
+                for i in range(2):
+                    words = raw[c][:, i, :].bitcast(F32)
+                    for u in range(2):
+                        nc.tensor.transpose(bank[:, u, P * i : P * i + P], words[:, 256 * f + u : 256 * f + 256 : 2], ident[:])
+
+        def Z(c):
+            rows_to_banks(z_raw, t_z, c, "tr")
+
+        def A(c):
+            rows_to_banks(a_raw, t_a, c, "a")
+
+        def Zc(c):
+            for f in range(2):
+                z_bf[c, f] = work.tile([P, CH, 4], BF16, name="z_bf", align_bytes=64, bufs=4)
+                nc.scalar.copy(out=z_bf[c, f][:].rearrange("p n t -> p (n t)").bitcast(F32).rearrange("p (n u) -> p n u", u=2), in_=t_z[c, f][:].rearrange("p u n -> p n u"))
+
+        def Zq(c):
+            for f in range(2):
+                z_codes[c, f] = work.tile([P, CH], U32, name="z_codes", align_bytes=64, bufs=6)
+                z_scales[c, f] = work.tile([P, CH], U8, name="z_scales", align_bytes=64, bufs=6)
+                nc.vector.quantize_mx(out=z_codes[c, f][:].bitcast(FP8X4), scales=z_scales[c, f][:], in_=z_bf[c, f][:].rearrange("p n t -> p (n t)"))
+
+        def YRs(G, slots):
+            for j in slots:
+                nc.vector.tensor_scalar_mul(y_scaled[G][:, j, :], y_raw[G, j][:], vecs["r"][:, G, j : j + 1])
+
+        def YRi(G, h, parts):
+            for k in parts:
+                cols = slice(512 * h + 256 * k, 512 * h + 256 * k + 256)
+                nc.scalar.copy(out=yr_bf[G][:, cols, :].rearrange("p (c i) t -> p c t i", i=4), in_=y_scaled[G][:, :, cols].rearrange("p t (c i) -> p c t i", i=4))
+
+        def YRq(G, h):
+            cols = slice(512 * h, 512 * h + 512)
+            nc.vector.quantize_mx(out=yr_codes[G][:, cols].bitcast(FP8X4), scales=yr_scales[G][:, cols], in_=yr_bf[G][:, cols, :].rearrange("p d t -> p (d t)"))
+
+        def S1(c, G):
+            for tp in range(2):
+                bank = psum.tile([P, 2, CH], F32, name="bank_s", tag="s")
+                t_s[c, G, tp] = bank
+                for k in range(2):
+                    m0 = 512 * G + P * (2 * tp + k)
+                    for f in range(2):
+                        nc.tensor.matmul_mx(out=bank[:, k, :], lhsT=yg_codes[f][:, m0 : m0 + P].bitcast(FP8X4), lhsT_scale=yg_scales[f][:, m0 : m0 + P], rhs=z_codes[c, f][:].bitcast(FP8X4), rhs_scale=z_scales[c, f][:], start=(f == 0), stop=(f == 1))
+
+        def Pr(c, G):
+            pr[c, G] = work.tile([P, 4, CH], F32, name="pr", bufs=4)
+            for t in range(4):
+                nc.scalar.activation(out=pr[c, G][:, t, :], in_=t_s[c, G, t // 2][:, t % 2, :], func=ACT.Sigmoid, bias=vecs["bj"][:, G, t : t + 1], scale=1.0 / 32.0)
+
+        def R(c, G):
+            dd[c, G] = work.tile([P, 4, CH], F32, name="dd", bufs=3)
+            nc.vector.tensor_tensor(
+                out=dd[c, G][:].rearrange("p (u e) n -> p u e n", u=2),
+                in0=pr[c, G][:].rearrange("p (u e) n -> p u e n", u=2),
+                in1=t_a[c, G][:].rearrange("p u n -> p (u n)").bitcast(BF16).rearrange("p (u n e) -> p u e n", u=2, e=2),
+                op=ALU.subtract,
+            )
+
+        def Mu(c, G):
+            res_bf[c, G] = work.tile([P, CH, 4], BF16, name="res_bf", align_bytes=64, bufs=3)
+            nc.vector.tensor_tensor(
+                out=res_bf[c, G][:].rearrange("p (c i) t -> p c t i", i=4),
+                in0=dd[c, G][:].rearrange("p t (c i) -> p c t i", i=4),
+                in1=vecs["v"][:, G, :].unsqueeze(1).unsqueeze(3).to_broadcast([P, CH // 4, 4, 4]),
+                op=ALU.mult,
+            )
+
+        def Rq(c, G):
+            res_codes[c, G] = work.tile([P, CH], U32, name="res_codes", align_bytes=64, bufs=8)
+            res_scales[c, G] = work.tile([P, CH], U8, name="res_scales", align_bytes=64, bufs=8)
+            nc.vector.quantize_mx(out=res_codes[c, G][:].bitcast(FP8X4), scales=res_scales[c, G][:], in_=res_bf[c, G][:].rearrange("p n t -> p (n t)"))
+
+        def O(c, i):
+            for h in range(2):
+                bank = psum.tile([P, 512], F32, name="bank_o", tag="o")
+                t_o[c, i, h] = bank
+                for G in range(2):
+                    nc.tensor.matmul_mx(out=bank[:], lhsT=res_codes[c, G][:, P * i : P * i + P].bitcast(FP8X4), lhsT_scale=res_scales[c, G][:, P * i : P * i + P], rhs=yr_codes[G][:, 512 * h : 512 * h + 512].bitcast(FP8X4), rhs_scale=yr_scales[G][:, 512 * h : 512 * h + 512], start=(G == 0), stop=(G == 1))
+
+        def Oe(c, i, engines="SS"):
+            of[c, i] = work.tile([P, D], F32, name="of", bufs=6)
+            for h in range(2):
+                dst = of[c, i][:, 512 * h : 512 * h + 512]
+                if engines[h] == "S":
+                    nc.scalar.mul(dst, t_o[c, i, h][:], 1.0 / 32.0)
+                else:
+                    nc.vector.tensor_scalar_mul(dst, t_o[c, i, h][:], 1.0 / 32.0)
+            n0 = CH * c + P * i
+            nc.sync.dma_start(out=out_0[n0 : n0 + P, :], in_=of[c, i][:])
+
+        def C(c, i):
+            cast[c, i] = work.tile([P, D], BF16, name="cast", align_bytes=64, bufs=6)
+            nc.vector.tensor_copy(out=cast[c, i][:].rearrange("p (u q e) -> p u q e", u=2, e=2), in_=of[c, i][:].rearrange("p (q u e) -> p u q e", u=2, e=2))
+
+        def Pt(c):
+            for f in range(2):
+                bank = psum.tile([P, 2, CH], F32, name="bank_tr", tag="tr")
+                t_p[c, f] = bank
+                for i in range(2):
+                    words = cast[c, i][:].bitcast(F32)
+                    for u in range(2):
+                        w0 = 256 * u + P * f
+                        nc.tensor.transpose(bank[:, u, P * i : P * i + P], words[:, w0 : w0 + P], ident[:])
+
+        def Pc(c, engines="SS"):
+            for f in range(2):
+                p_bf[c, f] = work.tile([P, CH, 4], BF16, name="p_bf", align_bytes=64, bufs=4)
+                dst = p_bf[c, f][:].rearrange("p n t -> p (n t)").bitcast(F32).rearrange("p (n u) -> p n u", u=2)
+                src = t_p[c, f][:].rearrange("p u n -> p n u")
+                if engines[f] == "S":
+                    nc.scalar.copy(out=dst, in_=src)
+                else:
+                    nc.vector.tensor_copy(out=dst, in_=src)
+
+        def Pq(c):
+            n0 = CH * c
+            for f in range(2):
+                p_codes[c, f] = work.tile([P, CH], U32, name="p_codes", align_bytes=64, bufs=4)
+                nc.vector.quantize_mx(out=p_codes[c, f][:].bitcast(FP8X4), scales=out_scales[:, f, n0 : n0 + CH], in_=p_bf[c, f][:].rearrange("p n t -> p (n t)"))
+                nc.sync.dma_start(out=out_1[f, :, n0 : n0 + CH, :].rearrange("p n t -> p (n t)").bitcast(I32), in_=p_codes[c, f][:].bitcast(I32))
+
+        def store_scales(n0, n1):
+            for Q in range(4):
+                nc.sync.dma_start(out=out_2[:, 4 * Q : 4 * Q + 4, n0:n1].rearrange("f q n -> q f n").bitcast(I32), in_=out_scales[32 * Q : 32 * Q + 4, :, n0:n1].bitcast(I32))
+
+        def RM(c):
+            R(c, 0)
+            R(c, 1)
+            Mu(c, 0)
+            Mu(c, 1)
+
+        def RQ(c):
+            Rq(c, 0)
+            Rq(c, 1)
+
+        with tc.manual_schedule():
+            for name, src in (("r", r), ("g", g), ("bj", bj), ("v", v)):
+                nc.scalar.dma_start(out=vecs[name][:], in_=src.rearrange("(G p t) -> p G t", p=P, t=4))
+            make_identity(nc, ident[:])
+            load_y(0)
+            load_y(1)
+            load_rows(z_raw, z, 0)
+            load_rows(z_raw, z, 1)
+            load_rows(a_raw, adj, 0)
+            load_rows(z_raw, z, 2)
+            load_rows(a_raw, adj, 1)
+            load_rows(z_raw, z, 3)
+            load_rows(a_raw, adj, 2)
+            load_rows(a_raw, adj, 3)
+            nc.scalar.activation(out=warm[:], in_=vecs["r"][:, 0, 0:1], func=ACT.Sigmoid)
+
+            YRs(0, (0, 1)); Y(0, 0); Ye(0, 0); YRs(0, (2, 3)); Y(0, 1); Ye(0, 1); YRi(0, 0, (0, 1)); Yq(0)
+            Y(1, 0); Ye(1, 0); Y(1, 1); Ye(1, 1)
+            Z(0); Zc(0); Yq(1); Zq(0); Z(1); Zc(1)
+            S1(0, 0); Pr(0, 0); YRs(1, (0, 1, 2, 3)); A(0); Zq(1); S1(0, 1); Pr(0, 1)
+            YRi(0, 1, (0,))
+            S1(1, 0); Pr(1, 0)
+            RM(0); Z(2); Zc(2); RQ(0)
+            S1(1, 1); A(1); Pr(1, 1); YRi(0, 1, (1,))
+            YRq(0, 0); Zq(2)
+            S1(2, 0); Pr(2, 0); YRi(1, 0, (0, 1))
+            RM(1); YRq(0, 1); RQ(1)
+            S1(2, 1); A(2); Z(3); Pr(2, 1); Zc(3); YRi(1, 1, (0, 1))
+            YRq(1, 0); Zq(3)
+            RM(2); YRq(1, 1); RQ(2)
+            S1(3, 0); Pr(3, 0); S1(3, 1); A(3); Pr(3, 1)
+            O(0, 0); Oe(0, 0); O(0, 1); Oe(0, 1)
+            RM(3); C(0, 0)
+            O(1, 0); Oe(1, 0); O(1, 1); Oe(1, 1)
+            RQ(3); C(0, 1)
+            O(2, 0); C(1, 0); Oe(2, 0); Pt(0); C(1, 1); Pc(0); O(2, 1); Oe(2, 1, "SV"); C(2, 0)
+            Pq(0)
+            O(3, 0); Oe(3, 0, "SV"); C(2, 1); Pt(1); Pc(1); O(3, 1); Pq(1); store_scales(0, 512); Oe(3, 1, "SV"); C(3, 0)
+            Pt(2); Pc(2); C(3, 1); Pt(3); Pq(2); Pc(3, "SV"); Pq(3); store_scales(512, 1024)

@@ -31,8 +31,8 @@ def tile_innerproductsigmoidresidualprojection_kernel(tc, z, y, adj, g, bj, v, r
         z_raw = {}
         a_raw = {}
         for G in range(2):
-            for j in range(4):
-                y_raw[G, j] = keep.tile([P, D], BF16, name="y_raw_%d_%d" % (G, j), align_bytes=64)
+            for jp in range(2):
+                y_raw[G, jp] = keep.tile([P, 2, D], BF16, name="y_raw_%d_%d" % (G, jp), align_bytes=64)
         for c in range(NCH):
             z_raw[c] = keep.tile([P, 2, D], BF16, name="z_raw_%d" % c, align_bytes=64)
             a_raw[c] = keep.tile([P, 2, M], BF16, name="a_raw_%d" % c, align_bytes=64)
@@ -57,15 +57,15 @@ def tile_innerproductsigmoidresidualprojection_kernel(tc, z, y, adj, g, bj, v, r
                 yg_bf[G, f] = keep.tile([P, 512, 4], BF16, name="yg_bf_%d_%d" % (G, f), align_bytes=64)
         out_scales = keep.tile([P, 2, N], U8, name="out_scales", align_bytes=64)
         ident = keep.tile([P, P], F32, name="ident")
+        r_f32 = keep.tile([P, 2, 4], F32, name="r_f32")
         warm = keep.tile([P, 1], F32, name="warm")
 
-        def load_y(G):
+        def load_y(G, jp):
             src = y[512 * G : 512 * G + 512, :].rearrange("(p j) d -> p j d", j=4)
-            for j in range(4):
-                nc.sync.dma_start(out=y_raw[G, j][:], in_=src[:, j, :])
+            nc.sync.dma_start(out=y_raw[G, jp][:], in_=src[:, 2 * jp : 2 * jp + 2, :])
 
         def load_rows(dst, src, c):
-            nc.sync.dma_start(out=dst[c][:], in_=src[CH * c : CH * c + CH, :].rearrange("(i p) k -> p i k", p=P))
+            nc.sync.dma_start(out=dst[c][:], in_=src[CH * c : CH * c + CH, :].rearrange("(p i) k -> p i k", i=2))
 
         t_y = {}
         t_z = {}
@@ -91,7 +91,7 @@ def tile_innerproductsigmoidresidualprojection_kernel(tc, z, y, adj, g, bj, v, r
                 bank = psum.tile([P, 2, CH], F32, name="bank_tr", tag="tr")
                 t_y[G, jp, f] = bank
                 for k in range(2):
-                    words = y_raw[G, 2 * jp + k][:].bitcast(F32)
+                    words = y_raw[G, jp][:, k, :].bitcast(F32)
                     for u in range(2):
                         nc.tensor.transpose(bank[:, u, P * k : P * k + P], words[:, 256 * f + u : 256 * f + 256 : 2], ident[:])
 
@@ -123,24 +123,30 @@ def tile_innerproductsigmoidresidualprojection_kernel(tc, z, y, adj, g, bj, v, r
             rows_to_banks(a_raw, t_a, c, "a")
 
         def Zc(c):
+            z_bf[c] = work.tile([P, 2, CH, 4], BF16, name="z_bf", align_bytes=64, bufs=2)
             for f in range(2):
-                z_bf[c, f] = work.tile([P, CH, 4], BF16, name="z_bf", align_bytes=64, bufs=4)
-                nc.scalar.copy(out=z_bf[c, f][:].rearrange("p n t -> p (n t)").bitcast(F32).rearrange("p (n u) -> p n u", u=2), in_=t_z[c, f][:].rearrange("p u n -> p n u"))
+                nc.scalar.copy(out=z_bf[c][:, f, :, :].rearrange("p n t -> p (n t)").bitcast(F32).rearrange("p (n u) -> p n u", u=2), in_=t_z[c, f][:].rearrange("p u n -> p n u"))
 
         def Zq(c):
-            for f in range(2):
-                z_codes[c, f] = work.tile([P, CH], U32, name="z_codes", align_bytes=64, bufs=6)
-                z_scales[c, f] = work.tile([P, CH], U8, name="z_scales", align_bytes=64, bufs=6)
-                nc.vector.quantize_mx(out=z_codes[c, f][:].bitcast(FP8X4), scales=z_scales[c, f][:], in_=z_bf[c, f][:].rearrange("p n t -> p (n t)"))
+            z_codes[c] = work.tile([P, 2 * CH], U32, name="z_codes", align_bytes=64, bufs=4)
+            z_scales[c] = work.tile([P, 2 * CH], U8, name="z_scales", align_bytes=64, bufs=4)
+            nc.vector.quantize_mx(out=z_codes[c][:].bitcast(FP8X4), scales=z_scales[c][:], in_=z_bf[c][:].rearrange("p f n t -> p (f n t)"))
 
-        def YRs(G, slots):
+        def YRs(G, slots, engine="V"):
             for j in slots:
-                nc.vector.tensor_scalar_mul(y_scaled[G][:, j, :], y_raw[G, j][:], vecs["r"][:, G, j : j + 1])
+                dst = y_scaled[G][:, j, :]
+                src = y_raw[G, j // 2][:, j % 2, :]
+                if engine == "V":
+                    nc.vector.tensor_scalar_mul(dst, src, vecs["r"][:, G, j : j + 1])
+                elif engine == "S":
+                    nc.scalar.activation(out=dst, in_=src, func=ACT.Copy, scale=r_f32[:, G, j : j + 1])
+                else:
+                    nc.gpsimd.tensor_scalar(out=dst, in0=src, scalar1=r_f32[:, G, j : j + 1], scalar2=0.0, op0=ALU.mult, op1=ALU.add)
 
-        def YRi(G, h, parts):
-            for k in parts:
+        def YRi(G, h, k, engine="S"):
                 cols = slice(512 * h + 256 * k, 512 * h + 256 * k + 256)
-                nc.scalar.copy(out=yr_bf[G][:, cols, :].rearrange("p (c i) t -> p c t i", i=4), in_=y_scaled[G][:, :, cols].rearrange("p t (c i) -> p c t i", i=4))
+                copy = nc.scalar.copy if engine == "S" else nc.vector.tensor_copy
+                copy(out=yr_bf[G][:, cols, :].rearrange("p (c i) t -> p c t i", i=4), in_=y_scaled[G][:, :, cols].rearrange("p t (c i) -> p c t i", i=4))
 
         def YRq(G, h):
             cols = slice(512 * h, 512 * h + 512)
@@ -153,7 +159,7 @@ def tile_innerproductsigmoidresidualprojection_kernel(tc, z, y, adj, g, bj, v, r
                 for k in range(2):
                     m0 = 512 * G + P * (2 * tp + k)
                     for f in range(2):
-                        nc.tensor.matmul_mx(out=bank[:, k, :], lhsT=yg_codes[f][:, m0 : m0 + P].bitcast(FP8X4), lhsT_scale=yg_scales[f][:, m0 : m0 + P], rhs=z_codes[c, f][:].bitcast(FP8X4), rhs_scale=z_scales[c, f][:], start=(f == 0), stop=(f == 1))
+                        nc.tensor.matmul_mx(out=bank[:, k, :], lhsT=yg_codes[f][:, m0 : m0 + P].bitcast(FP8X4), lhsT_scale=yg_scales[f][:, m0 : m0 + P], rhs=z_codes[c][:, CH * f : CH * f + CH].bitcast(FP8X4), rhs_scale=z_scales[c][:, CH * f : CH * f + CH], start=(f == 0), stop=(f == 1))
 
         def Pr(c, G):
             pr[c, G] = work.tile([P, 4, CH], F32, name="pr", bufs=4)
@@ -170,40 +176,45 @@ def tile_innerproductsigmoidresidualprojection_kernel(tc, z, y, adj, g, bj, v, r
             )
 
         def Mu(c, G):
-            res_bf[c, G] = work.tile([P, CH, 4], BF16, name="res_bf", align_bytes=64, bufs=3)
+            if c not in res_bf:
+                res_bf[c] = work.tile([P, 2, CH, 4], BF16, name="res_bf", align_bytes=64, bufs=2)
             nc.vector.tensor_tensor(
-                out=res_bf[c, G][:].rearrange("p (c i) t -> p c t i", i=4),
+                out=res_bf[c][:, G, :, :].rearrange("p (c i) t -> p c t i", i=4),
                 in0=dd[c, G][:].rearrange("p t (c i) -> p c t i", i=4),
                 in1=vecs["v"][:, G, :].unsqueeze(1).unsqueeze(3).to_broadcast([P, CH // 4, 4, 4]),
                 op=ALU.mult,
             )
 
-        def Rq(c, G):
-            res_codes[c, G] = work.tile([P, CH], U32, name="res_codes", align_bytes=64, bufs=8)
-            res_scales[c, G] = work.tile([P, CH], U8, name="res_scales", align_bytes=64, bufs=8)
-            nc.vector.quantize_mx(out=res_codes[c, G][:].bitcast(FP8X4), scales=res_scales[c, G][:], in_=res_bf[c, G][:].rearrange("p n t -> p (n t)"))
+        def Rq(c):
+            res_codes[c] = work.tile([P, 2 * CH], U32, name="res_codes", align_bytes=64, bufs=4)
+            res_scales[c] = work.tile([P, 2 * CH], U8, name="res_scales", align_bytes=64, bufs=4)
+            nc.vector.quantize_mx(out=res_codes[c][:].bitcast(FP8X4), scales=res_scales[c][:], in_=res_bf[c][:].rearrange("p f n t -> p (f n t)"))
 
         def O(c, i):
             for h in range(2):
                 bank = psum.tile([P, 512], F32, name="bank_o", tag="o")
                 t_o[c, i, h] = bank
                 for G in range(2):
-                    nc.tensor.matmul_mx(out=bank[:], lhsT=res_codes[c, G][:, P * i : P * i + P].bitcast(FP8X4), lhsT_scale=res_scales[c, G][:, P * i : P * i + P], rhs=yr_codes[G][:, 512 * h : 512 * h + 512].bitcast(FP8X4), rhs_scale=yr_scales[G][:, 512 * h : 512 * h + 512], start=(G == 0), stop=(G == 1))
+                    nc.tensor.matmul_mx(out=bank[:], lhsT=res_codes[c][:, CH * G + P * i : CH * G + P * i + P].bitcast(FP8X4), lhsT_scale=res_scales[c][:, CH * G + P * i : CH * G + P * i + P], rhs=yr_codes[G][:, 512 * h : 512 * h + 512].bitcast(FP8X4), rhs_scale=yr_scales[G][:, 512 * h : 512 * h + 512], start=(G == 0), stop=(G == 1))
 
         def Oe(c, i, engines="SS"):
-            of[c, i] = work.tile([P, D], F32, name="of", bufs=6)
+            of[c, i] = work.tile([P, D], F32, name="of", bufs=4)
             for h in range(2):
                 dst = of[c, i][:, 512 * h : 512 * h + 512]
                 if engines[h] == "S":
                     nc.scalar.mul(dst, t_o[c, i, h][:], 1.0 / 32.0)
                 else:
                     nc.vector.tensor_scalar_mul(dst, t_o[c, i, h][:], 1.0 / 32.0)
-            n0 = CH * c + P * i
-            nc.sync.dma_start(out=out_0[n0 : n0 + P, :], in_=of[c, i][:])
+            nc.sync.dma_start(out=out_0[CH * c : CH * c + CH, :].rearrange("(p i) d -> p i d", i=2)[:, i, :], in_=of[c, i][:])
 
-        def C(c, i):
-            cast[c, i] = work.tile([P, D], BF16, name="cast", align_bytes=64, bufs=6)
-            nc.vector.tensor_copy(out=cast[c, i][:].rearrange("p (u q e) -> p u q e", u=2, e=2), in_=of[c, i][:].rearrange("p (q u e) -> p u q e", u=2, e=2))
+        def C(c, i, engine="V"):
+            cast[c, i] = work.tile([P, D], BF16, name="cast", align_bytes=64, bufs=4)
+            dst = cast[c, i][:].rearrange("p (u q e) -> p u q e", u=2, e=2)
+            src = of[c, i][:].rearrange("p (q u e) -> p u q e", u=2, e=2)
+            if engine == "V":
+                nc.vector.tensor_copy(out=dst, in_=src)
+            else:
+                nc.gpsimd.tensor_scalar(out=dst, in0=src, scalar1=1.0, scalar2=0.0, op0=ALU.mult, op1=ALU.add)
 
         def Pt(c):
             for f in range(2):
@@ -216,42 +227,44 @@ def tile_innerproductsigmoidresidualprojection_kernel(tc, z, y, adj, g, bj, v, r
                         nc.tensor.transpose(bank[:, u, P * i : P * i + P], words[:, w0 : w0 + P], ident[:])
 
         def Pc(c, engines="SS"):
+            if c % 2 == 0:
+                p_bf[c // 2] = keep.tile([P, 2, 2 * CH, 4], BF16, name="p_bf_%d" % (c // 2), align_bytes=64)
+                p_codes[c // 2] = keep.tile([P, 2, 2 * CH], U32, name="p_codes_%d" % (c // 2), align_bytes=64)
+            n0 = CH * (c % 2)
             for f in range(2):
-                p_bf[c, f] = work.tile([P, CH, 4], BF16, name="p_bf", align_bytes=64, bufs=4)
-                dst = p_bf[c, f][:].rearrange("p n t -> p (n t)").bitcast(F32).rearrange("p (n u) -> p n u", u=2)
-                src = t_p[c, f][:].rearrange("p u n -> p n u")
+                dst = p_bf[c // 2][:, f, n0 : n0 + CH, :].rearrange("p n t -> p (n t)").bitcast(F32).rearrange("p (q i u) -> p q i u", i=2, u=2)
+                src = t_p[c, f][:].rearrange("p u (i q) -> p q i u", i=2)
                 if engines[f] == "S":
                     nc.scalar.copy(out=dst, in_=src)
                 else:
                     nc.vector.tensor_copy(out=dst, in_=src)
 
         def Pq(c):
-            n0 = CH * c
+            if c == 0:
+                return
+            h = c // 2
+            width = 2 * CH if c == 1 else CH
+            n0 = 0 if c == 1 else CH * (c % 2)
             for f in range(2):
-                p_codes[c, f] = work.tile([P, CH], U32, name="p_codes", align_bytes=64, bufs=4)
-                nc.vector.quantize_mx(out=p_codes[c, f][:].bitcast(FP8X4), scales=out_scales[:, f, n0 : n0 + CH], in_=p_bf[c, f][:].rearrange("p n t -> p (n t)"))
-                nc.sync.dma_start(out=out_1[f, :, n0 : n0 + CH, :].rearrange("p n t -> p (n t)").bitcast(I32), in_=p_codes[c, f][:].bitcast(I32))
-
-        def store_scales(n0, n1):
-            for Q in range(4):
-                nc.sync.dma_start(out=out_2[:, 4 * Q : 4 * Q + 4, n0:n1].rearrange("f q n -> q f n").bitcast(I32), in_=out_scales[32 * Q : 32 * Q + 4, :, n0:n1].bitcast(I32))
-
-        def RM(c):
-            R(c, 0)
-            R(c, 1)
-            Mu(c, 0)
-            Mu(c, 1)
-
-        def RQ(c):
-            Rq(c, 0)
-            Rq(c, 1)
+                nc.vector.quantize_mx(out=p_codes[h][:, f, n0 : n0 + width].bitcast(FP8X4), scales=out_scales[:, f, 512 * h + n0 : 512 * h + n0 + width], in_=p_bf[h][:, f, n0 : n0 + width, :].rearrange("p n t -> p (n t)"))
+                if c == 3:
+                    nc.sync.dma_start(out=out_1[f, :, 512 * h + n0 : 512 * h + n0 + width, :].rearrange("p n t -> p (n t)").bitcast(I32), in_=p_codes[h][:, f, n0 : n0 + width].bitcast(I32))
+            if c != 3:
+                nc.sync.dma_start(out=out_1[:, :, 512 * h + n0 : 512 * h + n0 + width, :].rearrange("f p n t -> p f (n t)").bitcast(I32), in_=p_codes[h][:, :, n0 : n0 + width].bitcast(I32))
+            if c == 3:
+                for Q in range(4):
+                    queue = nc.scalar if Q % 2 == 0 else nc.sync
+                    queue.dma_start(out=out_2[:, 4 * Q : 4 * Q + 4, :].rearrange("f q n -> q f n").bitcast(I32), in_=out_scales[32 * Q : 32 * Q + 4, :, :].bitcast(I32))
 
         with tc.manual_schedule():
             for name, src in (("r", r), ("g", g), ("bj", bj), ("v", v)):
                 nc.scalar.dma_start(out=vecs[name][:], in_=src.rearrange("(G p t) -> p G t", p=P, t=4))
             make_identity(nc, ident[:])
-            load_y(0)
-            load_y(1)
+            for j in range(2):
+                nc.sync.dma_start(out=y_raw[0, 0][:, j, :], in_=y[0:512, :].rearrange("(p j) d -> p j d", j=4)[:, j, :])
+            load_y(0, 1)
+            load_y(1, 0)
+            load_y(1, 1)
             load_rows(z_raw, z, 0)
             load_rows(z_raw, z, 1)
             load_rows(a_raw, adj, 0)
@@ -260,28 +273,25 @@ def tile_innerproductsigmoidresidualprojection_kernel(tc, z, y, adj, g, bj, v, r
             load_rows(z_raw, z, 3)
             load_rows(a_raw, adj, 2)
             load_rows(a_raw, adj, 3)
-            nc.scalar.activation(out=warm[:], in_=vecs["r"][:, 0, 0:1], func=ACT.Sigmoid)
+            nc.scalar.copy(out=r_f32[:], in_=vecs["r"][:])
+            nc.scalar.activation(out=warm[:], in_=r_f32[:, 0, 0:1], func=ACT.Sigmoid)
 
-            YRs(0, (0, 1)); Y(0, 0); Ye(0, 0); YRs(0, (2, 3)); Y(0, 1); Ye(0, 1); YRi(0, 0, (0, 1)); Yq(0)
-            Y(1, 0); Ye(1, 0); Y(1, 1); Ye(1, 1)
-            Z(0); Zc(0); Yq(1); Zq(0); Z(1); Zc(1)
-            S1(0, 0); Pr(0, 0); YRs(1, (0, 1, 2, 3)); A(0); Zq(1); S1(0, 1); Pr(0, 1)
-            YRi(0, 1, (0,))
-            S1(1, 0); Pr(1, 0)
-            RM(0); Z(2); Zc(2); RQ(0)
-            S1(1, 1); A(1); Pr(1, 1); YRi(0, 1, (1,))
-            YRq(0, 0); Zq(2)
-            S1(2, 0); Pr(2, 0); YRi(1, 0, (0, 1))
-            RM(1); YRq(0, 1); RQ(1)
-            S1(2, 1); A(2); Z(3); Pr(2, 1); Zc(3); YRi(1, 1, (0, 1))
-            YRq(1, 0); Zq(3)
-            RM(2); YRq(1, 1); RQ(2)
-            S1(3, 0); Pr(3, 0); S1(3, 1); A(3); Pr(3, 1)
-            O(0, 0); Oe(0, 0); O(0, 1); Oe(0, 1)
-            RM(3); C(0, 0)
-            O(1, 0); Oe(1, 0); O(1, 1); Oe(1, 1)
-            RQ(3); C(0, 1)
-            O(2, 0); C(1, 0); Oe(2, 0); Pt(0); C(1, 1); Pc(0); O(2, 1); Oe(2, 1, "SV"); C(2, 0)
-            Pq(0)
-            O(3, 0); Oe(3, 0, "SV"); C(2, 1); Pt(1); Pc(1); O(3, 1); Pq(1); store_scales(0, 512); Oe(3, 1, "SV"); C(3, 0)
-            Pt(2); Pc(2); C(3, 1); Pt(3); Pq(2); Pc(3, "SV"); Pq(3); store_scales(512, 1024)
+            Y(0, 0); YRs(0, (0, 1), "S"); Ye(0, 0); YRs(0, (2, 3)); Y(0, 1); Ye(0, 1)
+            Y(1, 0); Ye(1, 0); YRi(0, 1, 0); YRs(1, (2, 3)); Y(1, 1); YRi(0, 0, 1)
+            Ye(1, 1); YRs(1, (0, 1)); YRi(0, 0, 0); Yq(0); Z(0); YRi(0, 1, 1)
+            Zc(0); Zq(0); Yq(1); YRq(0, 0); Z(1); Zc(1)
+            S1(0, 0); Pr(0, 0); YRi(1, 0, 1); A(0); Zq(1); S1(0, 1)
+            R(0, 0); Z(2); Pr(0, 1); S1(1, 0); Zc(2); YRq(0, 1)
+            Pr(1, 0); Mu(0, 0); R(0, 1); A(1); S1(1, 1); Zq(2)
+            Mu(0, 1); Z(3); YRi(1, 0, 0); Pr(1, 1); R(1, 0); YRq(1, 0)
+            S1(2, 0); Zc(3); Mu(1, 0); R(1, 1); Zq(3); Pr(2, 0)
+            YRi(1, 1, 0); Rq(0); Mu(1, 1); S1(2, 1); A(2); Pr(2, 1)
+            R(2, 0); R(2, 1); S1(3, 0); A(3); YRi(1, 1, 1); Pr(3, 0)
+            YRq(1, 1); O(0, 0); S1(3, 1); Rq(1); Oe(0, 0); O(1, 1)
+            Pr(3, 1); Mu(2, 1); Mu(2, 0); R(3, 0); Oe(1, 1); O(0, 1)
+            C(0, 0); R(3, 1); Oe(0, 1); O(1, 0); Rq(2); Oe(1, 0)
+            Mu(3, 0); C(0, 1); Mu(3, 1); C(1, 0); O(2, 0); Pt(0)
+            C(1, 1); Rq(3); Oe(2, 0); O(2, 1); Pc(0); Pt(1)
+            Oe(2, 1); O(3, 0); C(2, 1); Pc(1, "SV"); C(2, 0); Pq(0)
+            Oe(3, 0); O(3, 1); C(3, 0); Pt(2); Oe(3, 1); C(3, 1)
+            Pc(2); Pt(3); Pq(1); Pq(2); Pc(3); Pq(3)

@@ -18,6 +18,7 @@ ALU = mybir.AluOpType
 P = 128
 CH = 256
 NCH = N // CH
+WIDE = (False, True)
 
 
 def tile_innerproductsigmoidresidualprojection_kernel(tc, z, y, adj, g, bj, v, r, out_0, out_1, out_2):
@@ -30,12 +31,6 @@ def tile_innerproductsigmoidresidualprojection_kernel(tc, z, y, adj, g, bj, v, r
         y_raw = {}
         z_raw = {}
         a_raw = {}
-        for G in range(2):
-            for jp in range(2):
-                y_raw[G, jp] = keep.tile([P, 2, D], BF16, name="y_raw_%d_%d" % (G, jp), align_bytes=64)
-        for c in range(NCH):
-            z_raw[c] = keep.tile([P, 2, D], BF16, name="z_raw_%d" % c, align_bytes=64)
-            a_raw[c] = keep.tile([P, 2, M], BF16, name="a_raw_%d" % c, align_bytes=64)
         vecs = {}
         for name in ("r", "g", "bj", "v"):
             vecs[name] = keep.tile([P, 2, 4], BF16, name="vec_" + name)
@@ -53,18 +48,21 @@ def tile_innerproductsigmoidresidualprojection_kernel(tc, z, y, adj, g, bj, v, r
             yr_scales[G] = keep.tile([P, D], U8, name="yr_scales_%d" % G, align_bytes=64)
             yg_codes[G] = keep.tile([P, M], U32, name="yg_codes_%d" % G, align_bytes=64)
             yg_scales[G] = keep.tile([P, M], U8, name="yg_scales_%d" % G, align_bytes=64)
-            for f in range(2):
-                yg_bf[G, f] = keep.tile([P, 512, 4], BF16, name="yg_bf_%d_%d" % (G, f), align_bytes=64)
         out_scales = keep.tile([P, 2, N], U8, name="out_scales", align_bytes=64)
         ident = keep.tile([P, P], F32, name="ident")
         r_f32 = keep.tile([P, 2, 4], F32, name="r_f32")
         warm = keep.tile([P, 1], F32, name="warm")
 
+        def new_raw():
+            return work.tile([P, 2, D], BF16, name="raw", align_bytes=64, bufs=10)
+
         def load_y(G, jp):
+            y_raw[G, jp] = new_raw()
             src = y[512 * G : 512 * G + 512, :].rearrange("(p j) d -> p j d", j=4)
             nc.sync.dma_start(out=y_raw[G, jp][:], in_=src[:, 2 * jp : 2 * jp + 2, :])
 
         def load_rows(dst, src, c):
+            dst[c] = new_raw()
             nc.sync.dma_start(out=dst[c][:], in_=src[CH * c : CH * c + CH, :].rearrange("(p i) k -> p i k", i=2))
 
         t_y = {}
@@ -97,6 +95,8 @@ def tile_innerproductsigmoidresidualprojection_kernel(tc, z, y, adj, g, bj, v, r
 
         def Ye(G, jp):
             for f in range(2):
+                if jp == 0:
+                    yg_bf[G, f] = work.tile([P, 512, 4], BF16, name="yg_bf", tag="f4k", align_bytes=64, bufs=4)
                 src = t_y[G, jp, f][:].rearrange("p u m -> p (u m)").bitcast(BF16).rearrange("p (u m e) -> p m u e", u=2, e=2)
                 dst = yg_bf[G, f][:, CH * jp : CH * jp + CH, :].rearrange("p m (u e) -> p m u e", u=2)
                 fac = vecs["g"][:, f, :].unsqueeze(1).to_broadcast([P, CH, 4]).rearrange("p m (u e) -> p m u e", u=2)
@@ -122,15 +122,24 @@ def tile_innerproductsigmoidresidualprojection_kernel(tc, z, y, adj, g, bj, v, r
         def A(c):
             rows_to_banks(a_raw, t_a, c, "a")
 
+        def z_slot(c, f):
+            h, k = divmod(c, 2)
+            return 2 * f + k if WIDE[h] else 2 * k + f
+
         def Zc(c):
-            z_bf[c] = work.tile([P, 2, CH, 4], BF16, name="z_bf", align_bytes=64, bufs=2)
+            h, k = divmod(c, 2)
+            if k == 0:
+                z_bf[h] = work.tile([P, 4, CH, 4], BF16, name="z_bf", align_bytes=64, bufs=2)
             for f in range(2):
-                nc.scalar.copy(out=z_bf[c][:, f, :, :].rearrange("p n t -> p (n t)").bitcast(F32).rearrange("p (n u) -> p n u", u=2), in_=t_z[c, f][:].rearrange("p u n -> p n u"))
+                nc.scalar.copy(out=z_bf[h][:, z_slot(c, f), :, :].rearrange("p n t -> p (n t)").bitcast(F32).rearrange("p (n u) -> p n u", u=2), in_=t_z[c, f][:].rearrange("p u n -> p n u"))
 
         def Zq(c):
-            z_codes[c] = work.tile([P, 2 * CH], U32, name="z_codes", align_bytes=64, bufs=4)
-            z_scales[c] = work.tile([P, 2 * CH], U8, name="z_scales", align_bytes=64, bufs=4)
-            nc.vector.quantize_mx(out=z_codes[c][:].bitcast(FP8X4), scales=z_scales[c][:], in_=z_bf[c][:].rearrange("p f n t -> p (f n t)"))
+            h, k = divmod(c, 2)
+            if k == 0:
+                z_codes[h] = work.tile([P, 4 * CH], U32, name="z_codes", align_bytes=64, bufs=2)
+                z_scales[h] = work.tile([P, 4 * CH], U8, name="z_scales", align_bytes=64, bufs=2)
+            cols = slice(2 * CH * k, 2 * CH * k + 2 * CH)
+            nc.vector.quantize_mx(out=z_codes[h][:, cols].bitcast(FP8X4), scales=z_scales[h][:, cols], in_=z_bf[h][:, 2 * k : 2 * k + 2, :, :].rearrange("p s n t -> p (s n t)"))
 
         def YRs(G, slots, engine="V"):
             for j in slots:
@@ -153,24 +162,39 @@ def tile_innerproductsigmoidresidualprojection_kernel(tc, z, y, adj, g, bj, v, r
             nc.vector.quantize_mx(out=yr_codes[G][:, cols].bitcast(FP8X4), scales=yr_scales[G][:, cols], in_=yr_bf[G][:, cols, :].rearrange("p d t -> p (d t)"))
 
         def S1(c, G):
+            h = c // 2
+            if WIDE[h]:
+                if c % 2 == 1:
+                    return
+                pr[h, G] = work.tile([P, 4, 2 * CH], F32, name="pr_wide", bufs=2)
+                for t in range(4):
+                    bank = psum.tile([P, 2 * CH], F32, name="bank_s", tag="s")
+                    m0 = 512 * G + P * t
+                    for f in range(2):
+                        nc.tensor.matmul_mx(out=bank[:], lhsT=yg_codes[f][:, m0 : m0 + P].bitcast(FP8X4), lhsT_scale=yg_scales[f][:, m0 : m0 + P], rhs=z_codes[h][:, 512 * f : 512 * f + 512].bitcast(FP8X4), rhs_scale=z_scales[h][:, 512 * f : 512 * f + 512], start=(f == 0), stop=(f == 1))
+                    nc.scalar.activation(out=pr[h, G][:, t, :], in_=bank[:], func=ACT.Sigmoid, bias=vecs["bj"][:, G, t : t + 1], scale=1.0 / 32.0)
+                return
             for tp in range(2):
                 bank = psum.tile([P, 2, CH], F32, name="bank_s", tag="s")
                 t_s[c, G, tp] = bank
                 for k in range(2):
                     m0 = 512 * G + P * (2 * tp + k)
                     for f in range(2):
-                        nc.tensor.matmul_mx(out=bank[:, k, :], lhsT=yg_codes[f][:, m0 : m0 + P].bitcast(FP8X4), lhsT_scale=yg_scales[f][:, m0 : m0 + P], rhs=z_codes[c][:, CH * f : CH * f + CH].bitcast(FP8X4), rhs_scale=z_scales[c][:, CH * f : CH * f + CH], start=(f == 0), stop=(f == 1))
+                        nc.tensor.matmul_mx(out=bank[:, k, :], lhsT=yg_codes[f][:, m0 : m0 + P].bitcast(FP8X4), lhsT_scale=yg_scales[f][:, m0 : m0 + P], rhs=z_codes[h][:, CH * z_slot(c, f) : CH * z_slot(c, f) + CH].bitcast(FP8X4), rhs_scale=z_scales[h][:, CH * z_slot(c, f) : CH * z_slot(c, f) + CH], start=(f == 0), stop=(f == 1))
 
         def Pr(c, G):
-            pr[c, G] = work.tile([P, 4, CH], F32, name="pr", bufs=4)
+            if WIDE[c // 2]:
+                return
+            pr[c, G, "n"] = work.tile([P, 4, CH], F32, name="pr", bufs=4)
             for t in range(4):
-                nc.scalar.activation(out=pr[c, G][:, t, :], in_=t_s[c, G, t // 2][:, t % 2, :], func=ACT.Sigmoid, bias=vecs["bj"][:, G, t : t + 1], scale=1.0 / 32.0)
+                nc.scalar.activation(out=pr[c, G, "n"][:, t, :], in_=t_s[c, G, t // 2][:, t % 2, :], func=ACT.Sigmoid, bias=vecs["bj"][:, G, t : t + 1], scale=1.0 / 32.0)
 
         def R(c, G):
+            prob = pr[c // 2, G][:, :, CH * (c % 2) : CH * (c % 2) + CH] if WIDE[c // 2] else pr[c, G, "n"][:]
             dd[c, G] = work.tile([P, 4, CH], F32, name="dd", bufs=3)
             nc.vector.tensor_tensor(
                 out=dd[c, G][:].rearrange("p (u e) n -> p u e n", u=2),
-                in0=pr[c, G][:].rearrange("p (u e) n -> p u e n", u=2),
+                in0=prob.rearrange("p (u e) n -> p u e n", u=2),
                 in1=t_a[c, G][:].rearrange("p u n -> p (u n)").bitcast(BF16).rearrange("p (u n e) -> p u e n", u=2, e=2),
                 op=ALU.subtract,
             )
@@ -198,7 +222,7 @@ def tile_innerproductsigmoidresidualprojection_kernel(tc, z, y, adj, g, bj, v, r
                     nc.tensor.matmul_mx(out=bank[:], lhsT=res_codes[c][:, CH * G + P * i : CH * G + P * i + P].bitcast(FP8X4), lhsT_scale=res_scales[c][:, CH * G + P * i : CH * G + P * i + P], rhs=yr_codes[G][:, 512 * h : 512 * h + 512].bitcast(FP8X4), rhs_scale=yr_scales[G][:, 512 * h : 512 * h + 512], start=(G == 0), stop=(G == 1))
 
         def Oe(c, i, engines="SS"):
-            of[c, i] = work.tile([P, D], F32, name="of", bufs=4)
+            of[c, i] = work.tile([P, D], F32, name="of", tag="f4k", align_bytes=64, bufs=4)
             for h in range(2):
                 dst = of[c, i][:, 512 * h : 512 * h + 512]
                 if engines[h] == "S":
@@ -209,6 +233,10 @@ def tile_innerproductsigmoidresidualprojection_kernel(tc, z, y, adj, g, bj, v, r
 
         def C(c, i, engine="V"):
             cast[c, i] = work.tile([P, D], BF16, name="cast", align_bytes=64, bufs=4)
+            if engine == "S":
+                for h in range(2):
+                    nc.scalar.mul(cast[c, i][:].rearrange("p (u h q e) -> p h u q e", u=2, h=2, e=2)[:, h, :, :, :], t_o[c, i, h][:].rearrange("p (q u e) -> p u q e", u=2, e=2), 1.0 / 32.0)
+                return
             dst = cast[c, i][:].rearrange("p (u q e) -> p u q e", u=2, e=2)
             src = of[c, i][:].rearrange("p (q u e) -> p u q e", u=2, e=2)
             if engine == "V":
@@ -260,8 +288,10 @@ def tile_innerproductsigmoidresidualprojection_kernel(tc, z, y, adj, g, bj, v, r
             for name, src in (("r", r), ("g", g), ("bj", bj), ("v", v)):
                 nc.scalar.dma_start(out=vecs[name][:], in_=src.rearrange("(G p t) -> p G t", p=P, t=4))
             make_identity(nc, ident[:])
-            for j in range(2):
-                nc.sync.dma_start(out=y_raw[0, 0][:, j, :], in_=y[0:512, :].rearrange("(p j) d -> p j d", j=4)[:, j, :])
+            y_raw[0, 0] = new_raw()
+            for f in range(2):
+                cols = slice(512 * f, 512 * f + 512)
+                nc.sync.dma_start(out=y_raw[0, 0][:, :, cols], in_=y[0:512, cols].rearrange("(p j) d -> p j d", j=4)[:, 0:2, :])
             load_y(0, 1)
             load_y(1, 0)
             load_y(1, 1)
@@ -275,23 +305,26 @@ def tile_innerproductsigmoidresidualprojection_kernel(tc, z, y, adj, g, bj, v, r
             load_rows(a_raw, adj, 3)
             nc.scalar.copy(out=r_f32[:], in_=vecs["r"][:])
             nc.scalar.activation(out=warm[:], in_=r_f32[:, 0, 0:1], func=ACT.Sigmoid)
+            bank = psum.tile([P, 512], F32, name="bank_o", tag="o")
+            for k in range(14):
+                nc.tensor.transpose(bank[:, P * (k % 4) : P * (k % 4) + P], ident[:], ident[:])
 
-            Y(0, 0); YRs(0, (0, 1), "S"); Ye(0, 0); YRs(0, (2, 3)); Y(0, 1); Ye(0, 1)
-            Y(1, 0); Ye(1, 0); YRi(0, 1, 0); YRs(1, (2, 3)); Y(1, 1); YRi(0, 0, 1)
-            Ye(1, 1); YRs(1, (0, 1)); YRi(0, 0, 0); Yq(0); Z(0); YRi(0, 1, 1)
-            Zc(0); Zq(0); Yq(1); YRq(0, 0); Z(1); Zc(1)
-            S1(0, 0); Pr(0, 0); YRi(1, 0, 1); A(0); Zq(1); S1(0, 1)
-            R(0, 0); Z(2); Pr(0, 1); S1(1, 0); Zc(2); YRq(0, 1)
-            Pr(1, 0); Mu(0, 0); R(0, 1); A(1); S1(1, 1); Zq(2)
-            Mu(0, 1); Z(3); YRi(1, 0, 0); Pr(1, 1); R(1, 0); YRq(1, 0)
-            S1(2, 0); Zc(3); Mu(1, 0); R(1, 1); Zq(3); Pr(2, 0)
-            YRi(1, 1, 0); Rq(0); Mu(1, 1); S1(2, 1); A(2); Pr(2, 1)
-            R(2, 0); R(2, 1); S1(3, 0); A(3); YRi(1, 1, 1); Pr(3, 0)
-            YRq(1, 1); O(0, 0); S1(3, 1); Rq(1); Oe(0, 0); O(1, 1)
-            Pr(3, 1); Mu(2, 1); Mu(2, 0); R(3, 0); Oe(1, 1); O(0, 1)
-            C(0, 0); R(3, 1); Oe(0, 1); O(1, 0); Rq(2); Oe(1, 0)
-            Mu(3, 0); C(0, 1); Mu(3, 1); C(1, 0); O(2, 0); Pt(0)
-            C(1, 1); Rq(3); Oe(2, 0); O(2, 1); Pc(0); Pt(1)
-            Oe(2, 1); O(3, 0); C(2, 1); Pc(1, "SV"); C(2, 0); Pq(0)
-            Oe(3, 0); O(3, 1); C(3, 0); Pt(2); Oe(3, 1); C(3, 1)
-            Pc(2); Pt(3); Pq(1); Pq(2); Pc(3); Pq(3)
+            Y(0, 0); Ye(0, 0); Y(0, 1); YRs(0, (0, 1), "S"); YRs(0, (2, 3)); Ye(0, 1)
+            Y(1, 0); YRi(0, 0, 1); Ye(1, 0); YRi(0, 1, 0, "V"); Y(1, 1); Ye(1, 1)
+            YRs(1, (2, 3)); Z(0); A(0); Pq(0); YRi(0, 1, 1); YRs(1, (0, 1), "G")
+            Yq(0); YRi(0, 0, 0); S1(3, 1); Zc(0); Z(1); Zq(0)
+            YRi(1, 0, 1); YRq(0, 1); Zc(1); S1(0, 0); Yq(1); Pr(0, 0)
+            Z(2); YRi(1, 1, 1, "V"); S1(0, 1); Zc(2); YRq(0, 0); R(0, 0)
+            Pr(0, 1); Zq(1); Z(3); Zc(3); Mu(0, 0); Zq(2)
+            R(0, 1); S1(1, 1); Pr(1, 1); S1(1, 0); Pr(1, 0); Zq(3)
+            A(1); YRi(1, 0, 0); Mu(0, 1); Pr(2, 0); S1(2, 0); R(1, 0)
+            R(1, 1); YRq(1, 0); YRi(1, 1, 0); Rq(0); Mu(1, 0); A(2)
+            R(2, 0); S1(2, 1); YRq(1, 1); O(0, 0); S1(3, 0); Oe(0, 0)
+            O(0, 1); Mu(2, 0); Mu(1, 1); Pr(3, 1); Oe(0, 1); R(2, 1)
+            C(0, 1, "S"); Rq(1); A(3); O(1, 0); Oe(1, 0); O(1, 1)
+            Oe(1, 1); Mu(2, 1); Pr(2, 1); C(0, 0, "G"); R(3, 0); Rq(2)
+            O(2, 0); Pt(0); Oe(2, 0); O(2, 1); C(1, 0, "G"); R(3, 1)
+            Pc(0); Mu(3, 0); Mu(3, 1); C(1, 1); Pt(1); Oe(2, 1)
+            Pc(1); Rq(3); C(2, 0); O(3, 0); Oe(3, 0, "VS"); C(2, 1, "G")
+            Pq(1); O(3, 1); Pt(2); C(3, 0); Oe(3, 1); C(3, 1)
+            Pc(2); Pt(3); Pc(3); Pq(2); Pq(3); Pr(3, 0)

from contextlib import ExitStack

import concourse.mybir as mybir
from concourse.masks import make_identity

N, M, D = 1024, 1024, 1024
FLOPS = 2 * N * M * D + 2 * N * M * D

F32 = mybir.dt.float32
BF16 = mybir.dt.bfloat16
U32 = mybir.dt.uint32
I32 = mybir.dt.int32
U8 = mybir.dt.uint8
FP8X4 = mybir.dt.float8_e4m3fn_x4
ACT = mybir.ActivationFunctionType
ALU = mybir.AluOpType

P = 128
CH = 256
NCH = N // CH
WIDE = (False, True)


def tile_innerproductsigmoidresidualprojection_kernel(tc, z, y, adj, g, bj, v, r, out_0, out_1, out_2):
    nc = tc.nc
    with ExitStack() as ctx:
        keep = ctx.enter_context(tc.tile_pool(name="keep", bufs=1))
        work = ctx.enter_context(tc.tile_pool(name="work", bufs=2))
        psum = ctx.enter_context(tc.psum_pool(name="psum", bufs=2))

        y_raw = {}
        z_raw = {}
        a_raw = {}
        vecs = {}
        for name in ("r", "g", "bj", "v"):
            vecs[name] = keep.tile([P, 2, 4], BF16, name="vec_" + name)
        y_scaled = {}
        yr_bf = {}
        yr_codes = {}
        yr_scales = {}
        yg_bf = {}
        yg_codes = {}
        yg_scales = {}
        for G in range(2):
            y_scaled[G] = keep.tile([P, 4, D], BF16, name="y_scaled_%d" % G, align_bytes=64)
            yr_bf[G] = keep.tile([P, D, 4], BF16, name="yr_bf_%d" % G, align_bytes=64)
            yr_codes[G] = keep.tile([P, D], U32, name="yr_codes_%d" % G, align_bytes=64)
            yr_scales[G] = keep.tile([P, D], U8, name="yr_scales_%d" % G, align_bytes=64)
            yg_codes[G] = keep.tile([P, M], U32, name="yg_codes_%d" % G, align_bytes=64)
            yg_scales[G] = keep.tile([P, M], U8, name="yg_scales_%d" % G, align_bytes=64)
        out_scales = keep.tile([P, 2, N], U8, name="out_scales", align_bytes=64)
        ident = keep.tile([P, P], F32, name="ident")
        r_f32 = keep.tile([P, 2, 4], F32, name="r_f32")
        warm = keep.tile([P, 1], F32, name="warm")

        def new_raw():
            return work.tile([P, 2, D], BF16, name="raw", align_bytes=64, bufs=10)

        def load_y(G, jp):
            y_raw[G, jp] = new_raw()
            src = y[512 * G : 512 * G + 512, :].rearrange("(p j) d -> p j d", j=4)
            nc.sync.dma_start(out=y_raw[G, jp][:], in_=src[:, 2 * jp : 2 * jp + 2, :])

        def load_rows(dst, src, c):
            dst[c] = new_raw()
            nc.sync.dma_start(out=dst[c][:], in_=src[CH * c : CH * c + CH, :].rearrange("(p i) k -> p i k", i=2))

        t_y = {}
        t_z = {}
        t_a = {}
        t_s = {}
        t_o = {}
        t_p = {}
        z_bf = {}
        z_codes = {}
        z_scales = {}
        pr = {}
        dd = {}
        res_bf = {}
        res_codes = {}
        res_scales = {}
        of = {}
        cast = {}
        p_bf = {}
        p_codes = {}

        def Y(G, jp):
            for f in range(2):
                bank = psum.tile([P, 2, CH], F32, name="bank_tr", tag="tr")
                t_y[G, jp, f] = bank
                for k in range(2):
                    words = y_raw[G, jp][:, k, :].bitcast(F32)
                    for u in range(2):
                        nc.tensor.transpose(bank[:, u, P * k : P * k + P], words[:, 256 * f + u : 256 * f + 256 : 2], ident[:])

        def Ye(G, jp):
            for f in range(2):
                if jp == 0:
                    yg_bf[G, f] = work.tile([P, 512, 4], BF16, name="yg_bf", tag="f4k", align_bytes=64, bufs=4)
                src = t_y[G, jp, f][:].rearrange("p u m -> p (u m)").bitcast(BF16).rearrange("p (u m e) -> p m u e", u=2, e=2)
                dst = yg_bf[G, f][:, CH * jp : CH * jp + CH, :].rearrange("p m (u e) -> p m u e", u=2)
                fac = vecs["g"][:, f, :].unsqueeze(1).to_broadcast([P, CH, 4]).rearrange("p m (u e) -> p m u e", u=2)
                nc.vector.tensor_tensor(out=dst, in0=src, in1=fac, op=ALU.mult)

        def Yq(G):
            cols = slice(512 * G, 512 * G + 512)
            for f in range(2):
                nc.vector.quantize_mx(out=yg_codes[f][:, cols].bitcast(FP8X4), scales=yg_scales[f][:, cols], in_=yg_bf[G, f][:].rearrange("p m t -> p (m t)"))

        def rows_to_banks(raw, store, c, tag):
            for f in range(2):
                bank = psum.tile([P, 2, CH], F32, name="bank_" + tag, tag=tag)
                store[c, f] = bank
                for i in range(2):
                    words = raw[c][:, i, :].bitcast(F32)
                    for u in range(2):
                        nc.tensor.transpose(bank[:, u, P * i : P * i + P], words[:, 256 * f + u : 256 * f + 256 : 2], ident[:])

        def Z(c):
            rows_to_banks(z_raw, t_z, c, "tr")

        def A(c):
            rows_to_banks(a_raw, t_a, c, "a")

        def z_slot(c, f):
            h, k = divmod(c, 2)
            return 2 * f + k if WIDE[h] else 2 * k + f

        def Zc(c):
            h, k = divmod(c, 2)
            if k == 0:
                z_bf[h] = work.tile([P, 4, CH, 4], BF16, name="z_bf", align_bytes=64, bufs=2)
            for f in range(2):
                nc.scalar.copy(out=z_bf[h][:, z_slot(c, f), :, :].rearrange("p n t -> p (n t)").bitcast(F32).rearrange("p (n u) -> p n u", u=2), in_=t_z[c, f][:].rearrange("p u n -> p n u"))

        def Zq(c):
            h, k = divmod(c, 2)
            if k == 0:
                z_codes[h] = work.tile([P, 4 * CH], U32, name="z_codes", align_bytes=64, bufs=2)
                z_scales[h] = work.tile([P, 4 * CH], U8, name="z_scales", align_bytes=64, bufs=2)
            cols = slice(2 * CH * k, 2 * CH * k + 2 * CH)
            nc.vector.quantize_mx(out=z_codes[h][:, cols].bitcast(FP8X4), scales=z_scales[h][:, cols], in_=z_bf[h][:, 2 * k : 2 * k + 2, :, :].rearrange("p s n t -> p (s n t)"))

        def YRs(G, slots, engine="V"):
            for j in slots:
                dst = y_scaled[G][:, j, :]
                src = y_raw[G, j // 2][:, j % 2, :]
                if engine == "V":
                    nc.vector.tensor_scalar_mul(dst, src, vecs["r"][:, G, j : j + 1])
                elif engine == "S":
                    nc.scalar.activation(out=dst, in_=src, func=ACT.Copy, scale=r_f32[:, G, j : j + 1])
                else:
                    nc.gpsimd.tensor_scalar(out=dst, in0=src, scalar1=r_f32[:, G, j : j + 1], scalar2=0.0, op0=ALU.mult, op1=ALU.add)

        def YRi(G, h, k, engine="S"):
                cols = slice(512 * h + 256 * k, 512 * h + 256 * k + 256)
                copy = nc.scalar.copy if engine == "S" else nc.vector.tensor_copy
                copy(out=yr_bf[G][:, cols, :].rearrange("p (c i) t -> p c t i", i=4), in_=y_scaled[G][:, :, cols].rearrange("p t (c i) -> p c t i", i=4))

        def YRq(G, h):
            cols = slice(512 * h, 512 * h + 512)
            nc.vector.quantize_mx(out=yr_codes[G][:, cols].bitcast(FP8X4), scales=yr_scales[G][:, cols], in_=yr_bf[G][:, cols, :].rearrange("p d t -> p (d t)"))

        def S1(c, G):
            h = c // 2
            if WIDE[h]:
                if c % 2 == 1:
                    return
                pr[h, G] = work.tile([P, 4, 2 * CH], F32, name="pr_wide", bufs=2)
                for t in range(4):
                    bank = psum.tile([P, 2 * CH], F32, name="bank_s", tag="s")
                    m0 = 512 * G + P * t
                    for f in range(2):
                        nc.tensor.matmul_mx(out=bank[:], lhsT=yg_codes[f][:, m0 : m0 + P].bitcast(FP8X4), lhsT_scale=yg_scales[f][:, m0 : m0 + P], rhs=z_codes[h][:, 512 * f : 512 * f + 512].bitcast(FP8X4), rhs_scale=z_scales[h][:, 512 * f : 512 * f + 512], start=(f == 0), stop=(f == 1))
                    nc.scalar.activation(out=pr[h, G][:, t, :], in_=bank[:], func=ACT.Sigmoid, bias=vecs["bj"][:, G, t : t + 1], scale=1.0 / 32.0)
                return
            for tp in range(2):
                bank = psum.tile([P, 2, CH], F32, name="bank_s", tag="s")
                t_s[c, G, tp] = bank
                for k in range(2):
                    m0 = 512 * G + P * (2 * tp + k)
                    for f in range(2):
                        nc.tensor.matmul_mx(out=bank[:, k, :], lhsT=yg_codes[f][:, m0 : m0 + P].bitcast(FP8X4), lhsT_scale=yg_scales[f][:, m0 : m0 + P], rhs=z_codes[h][:, CH * z_slot(c, f) : CH * z_slot(c, f) + CH].bitcast(FP8X4), rhs_scale=z_scales[h][:, CH * z_slot(c, f) : CH * z_slot(c, f) + CH], start=(f == 0), stop=(f == 1))

        def Pr(c, G):
            if WIDE[c // 2]:
                return
            pr[c, G, "n"] = work.tile([P, 4, CH], F32, name="pr", bufs=4)
            for t in range(4):
                nc.scalar.activation(out=pr[c, G, "n"][:, t, :], in_=t_s[c, G, t // 2][:, t % 2, :], func=ACT.Sigmoid, bias=vecs["bj"][:, G, t : t + 1], scale=1.0 / 32.0)

        def R(c, G):
            prob = pr[c // 2, G][:, :, CH * (c % 2) : CH * (c % 2) + CH] if WIDE[c // 2] else pr[c, G, "n"][:]
            dd[c, G] = work.tile([P, 4, CH], F32, name="dd", bufs=3)
            nc.vector.tensor_tensor(
                out=dd[c, G][:].rearrange("p (u e) n -> p u e n", u=2),
                in0=prob.rearrange("p (u e) n -> p u e n", u=2),
                in1=t_a[c, G][:].rearrange("p u n -> p (u n)").bitcast(BF16).rearrange("p (u n e) -> p u e n", u=2, e=2),
                op=ALU.subtract,
            )

        def Mu(c, G):
            if c not in res_bf:
                res_bf[c] = work.tile([P, 2, CH, 4], BF16, name="res_bf", align_bytes=64, bufs=2)
            nc.vector.tensor_tensor(
                out=res_bf[c][:, G, :, :].rearrange("p (c i) t -> p c t i", i=4),
                in0=dd[c, G][:].rearrange("p t (c i) -> p c t i", i=4),
                in1=vecs["v"][:, G, :].unsqueeze(1).unsqueeze(3).to_broadcast([P, CH // 4, 4, 4]),
                op=ALU.mult,
            )

        def Rq(c):
            res_codes[c] = work.tile([P, 2 * CH], U32, name="res_codes", align_bytes=64, bufs=4)
            res_scales[c] = work.tile([P, 2 * CH], U8, name="res_scales", align_bytes=64, bufs=4)
            nc.vector.quantize_mx(out=res_codes[c][:].bitcast(FP8X4), scales=res_scales[c][:], in_=res_bf[c][:].rearrange("p f n t -> p (f n t)"))

        def O(c, i):
            for h in range(2):
                bank = psum.tile([P, 512], F32, name="bank_o", tag="o")
                t_o[c, i, h] = bank
                for G in range(2):
                    nc.tensor.matmul_mx(out=bank[:], lhsT=res_codes[c][:, CH * G + P * i : CH * G + P * i + P].bitcast(FP8X4), lhsT_scale=res_scales[c][:, CH * G + P * i : CH * G + P * i + P], rhs=yr_codes[G][:, 512 * h : 512 * h + 512].bitcast(FP8X4), rhs_scale=yr_scales[G][:, 512 * h : 512 * h + 512], start=(G == 0), stop=(G == 1))

        def Oe(c, i, engines="SS"):
            of[c, i] = work.tile([P, D], F32, name="of", tag="f4k", align_bytes=64, bufs=4)
            for h in range(2):
                dst = of[c, i][:, 512 * h : 512 * h + 512]
                if engines[h] == "S":
                    nc.scalar.mul(dst, t_o[c, i, h][:], 1.0 / 32.0)
                else:
                    nc.vector.tensor_scalar_mul(dst, t_o[c, i, h][:], 1.0 / 32.0)
            nc.sync.dma_start(out=out_0[CH * c : CH * c + CH, :].rearrange("(p i) d -> p i d", i=2)[:, i, :], in_=of[c, i][:])

        def C(c, i, engine="V"):
            cast[c, i] = work.tile([P, D], BF16, name="cast", align_bytes=64, bufs=4)
            if engine == "S":
                for h in range(2):
                    nc.scalar.mul(cast[c, i][:].rearrange("p (u h q e) -> p h u q e", u=2, h=2, e=2)[:, h, :, :, :], t_o[c, i, h][:].rearrange("p (q u e) -> p u q e", u=2, e=2), 1.0 / 32.0)
                return
            dst = cast[c, i][:].rearrange("p (u q e) -> p u q e", u=2, e=2)
            src = of[c, i][:].rearrange("p (q u e) -> p u q e", u=2, e=2)
            if engine == "V":
                nc.vector.tensor_copy(out=dst, in_=src)
            else:
                nc.gpsimd.tensor_scalar(out=dst, in0=src, scalar1=1.0, scalar2=0.0, op0=ALU.mult, op1=ALU.add)

        def Pt(c):
            for f in range(2):
                bank = psum.tile([P, 2, CH], F32, name="bank_tr", tag="tr")
                t_p[c, f] = bank
                for i in range(2):
                    words = cast[c, i][:].bitcast(F32)
                    for u in range(2):
                        w0 = 256 * u + P * f
                        nc.tensor.transpose(bank[:, u, P * i : P * i + P], words[:, w0 : w0 + P], ident[:])

        def Pc(c, engines="SS"):
            if c % 2 == 0:
                p_bf[c // 2] = keep.tile([P, 2, 2 * CH, 4], BF16, name="p_bf_%d" % (c // 2), align_bytes=64)
                p_codes[c // 2] = keep.tile([P, 2, 2 * CH], U32, name="p_codes_%d" % (c // 2), align_bytes=64)
            n0 = CH * (c % 2)
            for f in range(2):
                dst = p_bf[c // 2][:, f, n0 : n0 + CH, :].rearrange("p n t -> p (n t)").bitcast(F32).rearrange("p (q i u) -> p q i u", i=2, u=2)
                src = t_p[c, f][:].rearrange("p u (i q) -> p q i u", i=2)
                if engines[f] == "S":
                    nc.scalar.copy(out=dst, in_=src)
                else:
                    nc.vector.tensor_copy(out=dst, in_=src)

        def Pq(c):
            if c == 0:
                return
            h = c // 2
            width = 2 * CH if c == 1 else CH
            n0 = 0 if c == 1 else CH * (c % 2)
            for f in range(2):
                nc.vector.quantize_mx(out=p_codes[h][:, f, n0 : n0 + width].bitcast(FP8X4), scales=out_scales[:, f, 512 * h + n0 : 512 * h + n0 + width], in_=p_bf[h][:, f, n0 : n0 + width, :].rearrange("p n t -> p (n t)"))
                if c == 3:
                    nc.sync.dma_start(out=out_1[f, :, 512 * h + n0 : 512 * h + n0 + width, :].rearrange("p n t -> p (n t)").bitcast(I32), in_=p_codes[h][:, f, n0 : n0 + width].bitcast(I32))
            if c != 3:
                nc.sync.dma_start(out=out_1[:, :, 512 * h + n0 : 512 * h + n0 + width, :].rearrange("f p n t -> p f (n t)").bitcast(I32), in_=p_codes[h][:, :, n0 : n0 + width].bitcast(I32))
            if c == 3:
                for Q in range(4):
                    queue = nc.scalar if Q % 2 == 0 else nc.sync
                    queue.dma_start(out=out_2[:, 4 * Q : 4 * Q + 4, :].rearrange("f q n -> q f n").bitcast(I32), in_=out_scales[32 * Q : 32 * Q + 4, :, :].bitcast(I32))

        with tc.manual_schedule():
            for name, src in (("r", r), ("g", g), ("bj", bj), ("v", v)):
                nc.scalar.dma_start(out=vecs[name][:], in_=src.rearrange("(G p t) -> p G t", p=P, t=4))
            make_identity(nc, ident[:])
            y_raw[0, 0] = new_raw()
            for f in range(2):
                cols = slice(512 * f, 512 * f + 512)
                nc.sync.dma_start(out=y_raw[0, 0][:, :, cols], in_=y[0:512, cols].rearrange("(p j) d -> p j d", j=4)[:, 0:2, :])
            load_y(0, 1)
            load_y(1, 0)
            load_y(1, 1)
            load_rows(z_raw, z, 0)
            load_rows(z_raw, z, 1)
            load_rows(a_raw, adj, 0)
            load_rows(z_raw, z, 2)
            load_rows(a_raw, adj, 1)
            load_rows(z_raw, z, 3)
            load_rows(a_raw, adj, 2)
            load_rows(a_raw, adj, 3)
            nc.scalar.copy(out=r_f32[:], in_=vecs["r"][:])
            nc.scalar.activation(out=warm[:], in_=r_f32[:, 0, 0:1], func=ACT.Sigmoid)
            bank = psum.tile([P, 512], F32, name="bank_o", tag="o")
            for k in range(14):
                nc.tensor.transpose(bank[:, P * (k % 4) : P * (k % 4) + P], ident[:], ident[:])

            Y(0, 0); Ye(0, 0); Y(0, 1); YRs(0, (0, 1), "S"); YRs(0, (2, 3)); Ye(0, 1)
            Y(1, 0); YRi(0, 0, 1); Ye(1, 0); YRi(0, 1, 0, "V"); Y(1, 1); Ye(1, 1)
            YRs(1, (2, 3)); Z(0); A(0); Pq(0); YRi(0, 1, 1); YRs(1, (0, 1), "G")
            Yq(0); YRi(0, 0, 0); S1(3, 1); Zc(0); Z(1); Zq(0)
            YRi(1, 0, 1); YRq(0, 1); Zc(1); S1(0, 0); Yq(1); Pr(0, 0)
            Z(2); YRi(1, 1, 1, "V"); S1(0, 1); Zc(2); YRq(0, 0); R(0, 0)
            Pr(0, 1); Zq(1); Z(3); Zc(3); Mu(0, 0); Zq(2)
            R(0, 1); S1(1, 1); Pr(1, 1); S1(1, 0); Pr(1, 0); Zq(3)
            A(1); YRi(1, 0, 0); Mu(0, 1); Pr(2, 0); S1(2, 0); R(1, 0)
            R(1, 1); YRq(1, 0); YRi(1, 1, 0); Rq(0); Mu(1, 0); A(2)
            R(2, 0); S1(2, 1); YRq(1, 1); O(0, 0); S1(3, 0); Oe(0, 0)
            O(0, 1); Mu(2, 0); Mu(1, 1); Pr(3, 1); Oe(0, 1); R(2, 1)
            C(0, 1, "S"); Rq(1); A(3); O(1, 0); Oe(1, 0); O(1, 1)
            Oe(1, 1); Mu(2, 1); Pr(2, 1); C(0, 0, "G"); R(3, 0); Rq(2)
            O(2, 0); Pt(0); Oe(2, 0); O(2, 1); C(1, 0, "G"); R(3, 1)
            Pc(0); Mu(3, 0); Mu(3, 1); C(1, 1); Pt(1); Oe(2, 1)
            Pc(1); Rq(3); C(2, 0); O(3, 0); Oe(3, 0, "VS"); C(2, 1, "G")
            Pq(1); O(3, 1); Pt(2); C(3, 0); Oe(3, 1); C(3, 1)
            Pc(2); Pt(3); Pc(3); Pq(2); Pq(3); Pr(3, 0)
